import numpy as np
import ml_dtypes


def mxq(x, axis, fmt="e4m3"):
    dtype, down = {"e4m3": (ml_dtypes.float8_e4m3fn, 7), "e5m2": (ml_dtypes.float8_e5m2, 14)}[fmt]
    v = np.moveaxis(np.asarray(x, np.float32).astype(ml_dtypes.bfloat16).astype(np.float64), axis, -1)
    blocks = v.reshape(v.shape[:-1] + (-1, 32))
    amax = np.abs(blocks).max(-1, keepdims=True)
    byte = np.maximum(np.where(amax > 0, np.frexp(amax)[1] - 1 + 127, 0) - down, 1)
    scale = np.exp2(byte - 127.0)
    codes = (blocks / scale).astype(np.float32).astype(dtype).astype(np.float64)
    return np.moveaxis((codes * scale).reshape(v.shape), -1, axis)


WIDE = False


def mx_kscale(k):
    if not WIDE:
        return np.ones(k)
    levels = np.array([10, -10, 5, -5, 0])
    if k % 512:
        return np.exp2(np.random.permutation(np.resize(levels, k // 32))).repeat(32)
    a = np.empty((k // 512, 16))
    for p in range(k // 512):
        a[p, :8] = np.random.permutation(np.resize(levels, 8))
        for g in range(8):
            far = levels[np.abs(levels - a[p, g]) >= 10]
            a[p, g + 8] = far[np.random.randint(len(far))]
    return np.exp2(a.ravel()).repeat(32)


def f64(x):
    return np.asarray(x).astype(np.float64)


E2M1 = np.array([0.0, 0.5, 1.0, 1.5, 2.0, 3.0, 4.0, 6.0, -0.0, -0.5, -1.0, -1.5, -2.0, -3.0, -4.0, -6.0])


def pack_weight(w, fmt):
    k, n = w.shape
    w = f64(np.asarray(w, np.float32).astype(ml_dtypes.bfloat16)).reshape(k // 32, 32, n)
    amax = np.abs(w).max(1)
    if fmt == "e4m3":
        byte = np.frexp(amax)[1] - 1 + 127 - 7
    else:
        mant, ex = np.frexp(amax / 6.0)
        byte = np.where(mant > 0.5, ex, ex - 1) + 127
    byte = np.clip(np.where(amax > 0, byte, 1), 1, 254)
    scaled = (w * np.exp2(127.0 - byte)[:, None, :]).reshape(k, n).astype(np.float32)
    by_word = np.ascontiguousarray(scaled.reshape(k // 512, 128, 4, n).transpose(0, 1, 3, 2))
    if fmt == "e4m3":
        words = by_word.astype(ml_dtypes.float8_e4m3fn).view(np.uint8)
    else:
        c = by_word.astype(ml_dtypes.float4_e2m1fn).view(np.uint8) & 0xF
        words = (c[..., 0::2] | (c[..., 1::2] << 4)).reshape(k // 512, 128, 2 * n)
    return np.ascontiguousarray(words), np.ascontiguousarray(byte.astype(np.uint8).reshape(k // 512, 16, n))


def unpack_weight(words, scales, fmt):
    g, _, n = scales.shape
    words = np.ascontiguousarray(words).reshape(g, 128, n, -1)
    if fmt == "e4m3":
        vals = words.view(ml_dtypes.float8_e4m3fn).astype(np.float64)
    else:
        nib = np.empty((g, 128, n, 4), np.uint8)
        nib[..., 0::2] = words & 0xF
        nib[..., 1::2] = words >> 4
        vals = E2M1[nib]
    vals = vals * np.repeat(np.exp2(scales.astype(np.float64) - 127.0), 8, axis=1)[..., None]
    return vals.transpose(0, 1, 3, 2).reshape(g * 512, n)


def silu(v):
    return v / (1.0 + np.exp(-v))


K, L, S, U, T, N = 1024, 512, 512, 512, 1024, 512


def setup_inputs():
    n = np.random.standard_normal
    fk = mx_kscale(K)
    fl = mx_kscale(L)
    xap = pack_weight(n((K, S)) / fk[:, None], "e4m3")
    wap = pack_weight(n((K, N)) * 1 / np.sqrt(K) * fk[:, None], "e2m1")
    wbp = pack_weight(n((K, N)) * 1 / np.sqrt(K) * fk[:, None], "e2m1")
    cxp = pack_weight(n((L, T)) / fl[:, None], "e2m1")
    wcp = pack_weight(n((L, N)) * 1 / np.sqrt(L) * fl[:, None], "e4m3")
    return {
        "xa_words": xap[0],
        "xa_scales": xap[1],
        "wa_words": wap[0],
        "wa_scales": wap[1],
        "xb": (n((K, U)) / fk[:, None]).astype(np.float32),
        "wb_words": wbp[0],
        "wb_scales": wbp[1],
        "cx_words": cxp[0],
        "cx_scales": cxp[1],
        "wc_words": wcp[0],
        "wc_scales": wcp[1],
    }


def reference(xa_words, xa_scales, wa_words, wa_scales, xb, wb_words, wb_scales, cx_words, cx_scales, wc_words, wc_scales):
    xau = unpack_weight(xa_words, xa_scales, "e4m3")
    wau = unpack_weight(wa_words, wa_scales, "e2m1")
    wbu = unpack_weight(wb_words, wb_scales, "e2m1")
    cxu = unpack_weight(cx_words, cx_scales, "e2m1")
    wcu = unpack_weight(wc_words, wc_scales, "e4m3")
    za = wau.T @ xau
    xbq = mxq(f64(xb), 0, "e4m3")
    zb = wbu.T @ xbq
    z = np.concatenate([za, zb], axis=1)
    p = wcu.T @ cxu
    y = silu(z + p)
    return y

@@ -1,0 +1,153 @@
+from contextlib import ExitStack
+
+import concourse.mybir as mybir
+
+K, L, S, U, T, N = 1024, 512, 512, 512, 1024, 512
+FLOPS = 2 * N * (K * S + K * U + L * T)
+
+F32 = mybir.dt.float32
+BF16 = mybir.dt.bfloat16
+I32 = mybir.dt.int32
+U32 = mybir.dt.uint32
+U8 = mybir.dt.uint8
+FP8X4 = mybir.dt.float8_e4m3fn_x4
+FP4X4 = mybir.dt.float4_e2m1fn_x4
+SILU = mybir.ActivationFunctionType.Silu
+
+P = 128
+PACK = 4
+K_PASS = P * PACK
+M_TILE = 128
+N_TILES = N // M_TILE
+HALF = U // 2
+
+
+def tile_mix_two_batches_one_context_kernel(
+    tc, xa_words, xa_scales, wa_words, wa_scales, xb, wb_words, wb_scales,
+    cx_words, cx_scales, wc_words, wc_scales, out
+):
+    nc = tc.nc
+    with ExitStack() as ctx:
+        keep = ctx.enter_context(tc.tile_pool(name="keep", bufs=1))
+        psum = ctx.enter_context(tc.psum_pool(name="psum", bufs=1))
+        ctx.enter_context(tc.manual_schedule())
+
+        groups = [[("wc", wc_scales), ("cx", cx_scales)], [("wa", wa_scales), ("xa", xa_scales), ("wb", wb_scales)]]
+        place = {}
+        staged = []
+        planes = []
+        for g, group in enumerate(groups):
+            width = 0
+            for name, src in group:
+                place[name] = (g, width)
+                width = width + src.shape[0] * src.shape[2]
+            staged.append(keep.tile([P, width], U8, align_bytes=64, name="staged%d" % g))
+            planes.append(keep.tile([P, width], U8, align_bytes=64, name="planes%d" % g))
+            nc.vector.memset(planes[g][:].bitcast(I32), 0)
+            for name, src in group:
+                z, c = src.shape[0], src.shape[2]
+                dst = staged[g][4:P:8, place[name][1] : place[name][1] + z * c].bitcast(I32)
+                nc.scalar.dma_start(
+                    out=dst.rearrange("q (z c) -> q z c", z=z),
+                    in_=src.bitcast(I32).rearrange("z q c -> q z c"),
+                )
+
+        def spread(g):
+            for r in range(4):
+                nc.sync.dma_start(
+                    out=planes[g][r:P:32, :].bitcast(I32),
+                    in_=staged[g][4 + 8 * r : P : 32, :].bitcast(I32),
+                )
+
+        wc = keep.tile([P, N], U32, align_bytes=64)
+        cx = keep.tile([P, 2 * T], U8, align_bytes=64)
+        wa = keep.tile([P, 2, 2 * N], U8, align_bytes=64)
+        xa = keep.tile([P, 2, S], U32, align_bytes=64)
+        wb = keep.tile([P, 2, 2 * N], U8, align_bytes=64)
+        xb_rows = xb.rearrange("(z p j) u -> z p j u", z=2, j=PACK)
+        raw0 = keep.tile([P, PACK, U], F32)
+        raw1a = keep.tile([P, PACK, HALF], F32)
+        raw1b = keep.tile([P, PACK, HALF], F32)
+        nc.sync.dma_start(out=wc[:].bitcast(I32), in_=wc_words[0].rearrange("p c r -> p (c r)").bitcast(I32))
+        nc.sync.dma_start(out=cx[:].bitcast(I32), in_=cx_words[0].bitcast(I32))
+        nc.sync.dma_start(
+            out=xa[:].bitcast(I32),
+            in_=xa_words.rearrange("z p c r -> z p (c r)").bitcast(I32).rearrange("z p c -> p z c"),
+        )
+        spread(0)
+        nc.sync.dma_start(out=wa[:].bitcast(I32), in_=wa_words.bitcast(I32).rearrange("z p c -> p z c"))
+        nc.sync.dma_start(out=raw0[:], in_=xb_rows[0])
+        spread(1)
+        nc.sync.dma_start(out=wb[:].bitcast(I32), in_=wb_words.bitcast(I32).rearrange("z p c -> p z c"))
+        nc.sync.dma_start(out=raw1a[:], in_=xb_rows[1][:, :, 0:HALF])
+        nc.sync.dma_start(out=raw1b[:], in_=xb_rows[1][:, :, HALF:U])
+
+        xq0 = keep.tile([P, U], U32, align_bytes=64)
+        xs0 = keep.tile([P, U], U8, align_bytes=64)
+        xq1 = keep.tile([P, U], U32, align_bytes=64)
+        xs1 = keep.tile([P, U], U8, align_bytes=64)
+
+        def interleave(raw, cols, name):
+            grouped = keep.tile([P, cols, PACK], BF16, align_bytes=64, name=name)
+            nc.vector.tensor_copy(
+                out=grouped[:].rearrange("p (c i) t -> p c t i", i=4),
+                in_=raw[:].rearrange("p t (c i) -> p c t i", i=4),
+            )
+            return grouped
+
+        def quantize(grouped, codes, scales):
+            nc.vector.quantize_mx(out=codes.bitcast(FP8X4), scales=scales, in_=grouped[:].rearrange("p c t -> p (c t)"))
+
+        g0 = interleave(raw0, U, "g0")
+        quantize(g0, xq0[:], xs0[:])
+        g1a = interleave(raw1a, HALF, "g1a")
+        quantize(g1a, xq1[:, 0:HALF], xs1[:, 0:HALF])
+        g1b = interleave(raw1b, HALF, "g1b")
+        quantize(g1b, xq1[:, HALF:U], xs1[:, HALF:U])
+
+        def plane(name, first, cols):
+            g, c0 = place[name]
+            return planes[g][:, c0 + first : c0 + first + cols]
+
+        def context_pass(acc, i, t0):
+            nc.tensor.matmul_mx(
+                out=acc[:],
+                lhsT=wc[:, M_TILE * i : M_TILE * (i + 1)].bitcast(FP8X4),
+                lhsT_scale=plane("wc", M_TILE * i, M_TILE),
+                rhs=cx[:, 2 * t0 : 2 * (t0 + S)].bitcast(FP4X4),
+                rhs_scale=plane("cx", t0, S),
+                start=True,
+                stop=False,
+            )
+
+        def batch_pass(acc, w, w_name, i, z, codes, scales):
+            nc.tensor.matmul_mx(
+                out=acc[:],
+                lhsT=w[:, z, 2 * M_TILE * i : 2 * M_TILE * (i + 1)].bitcast(FP4X4),
+                lhsT_scale=plane(w_name, N * z + M_TILE * i, M_TILE),
+                rhs=codes.bitcast(FP8X4),
+                rhs_scale=scales,
+                start=False,
+                stop=(z == 1),
+            )
+
+        def finish(acc, i, t0):
+            y = keep.tile([P, S], F32, name="y_%d_%d" % (t0, i))
+            nc.scalar.activation(out=y[:], in_=acc[:], func=SILU)
+            nc.sync.dma_start(out=out[M_TILE * i : M_TILE * (i + 1), t0 : t0 + S], in_=y[:])
+
+        acc_a = [psum.tile([P, S], F32, name="acc_a%d" % i) for i in range(N_TILES)]
+        acc_b = [psum.tile([P, U], F32, name="acc_b%d" % i) for i in range(N_TILES)]
+        for i in range(N_TILES):
+            context_pass(acc_a[i], i, 0)
+        for i in range(N_TILES):
+            context_pass(acc_b[i], i, S)
+        for i in range(N_TILES):
+            for z in range(2):
+                batch_pass(acc_a[i], wa, "wa", i, z, xa[:, z, :], plane("xa", S * z, S))
+            finish(acc_a[i], i, 0)
+        for i in range(N_TILES):
+            batch_pass(acc_b[i], wb, "wb", i, 0, xq0[:], xs0[:])
+        for i in range(N_TILES):
+            batch_pass(acc_b[i], wb, "wb", i, 1, xq1[:], xs1[:])
+            finish(acc_b[i], i, S)

@@ -20,6 +20,7 @@ K_PASS = P * PACK
 M_TILE = 128
 N_TILES = N // M_TILE
 HALF = U // 2
+SPLIT = 160
 
 
 def tile_mix_two_batches_one_context_kernel(
@@ -32,82 +33,76 @@ def tile_mix_two_batches_one_context_kernel(
         psum = ctx.enter_context(tc.psum_pool(name="psum", bufs=1))
         ctx.enter_context(tc.manual_schedule())
 
-        groups = [[("wc", wc_scales), ("cx", cx_scales)], [("wa", wa_scales), ("xa", xa_scales), ("wb", wb_scales)]]
-        place = {}
-        staged = []
-        planes = []
-        for g, group in enumerate(groups):
-            width = 0
-            for name, src in group:
-                place[name] = (g, width)
-                width = width + src.shape[0] * src.shape[2]
-            staged.append(keep.tile([P, width], U8, align_bytes=64, name="staged%d" % g))
-            planes.append(keep.tile([P, width], U8, align_bytes=64, name="planes%d" % g))
-            nc.vector.memset(planes[g][:].bitcast(I32), 0)
-            for name, src in group:
-                z, c = src.shape[0], src.shape[2]
-                dst = staged[g][4:P:8, place[name][1] : place[name][1] + z * c].bitcast(I32)
-                nc.scalar.dma_start(
-                    out=dst.rearrange("q (z c) -> q z c", z=z),
-                    in_=src.bitcast(I32).rearrange("z q c -> q z c"),
-                )
-
-        def spread(g):
-            for r in range(4):
-                nc.sync.dma_start(
-                    out=planes[g][r:P:32, :].bitcast(I32),
-                    in_=staged[g][4 + 8 * r : P : 32, :].bitcast(I32),
-                )
+        sources = [("wc", wc_scales), ("cx", cx_scales), ("wa", wa_scales), ("xa", xa_scales), ("wb", wb_scales)]
+        first_col = {}
+        width = 0
+        for name, src in sources:
+            first_col[name] = width
+            width = width + src.shape[0] * src.shape[2]
+        staged = keep.tile([P, width], U8, align_bytes=64)
+        planes = keep.tile([P, width], U8, align_bytes=64)
+        nc.vector.memset(planes[:].bitcast(I32), 0)
+        for n, (name, src) in enumerate(sources):
+            z, c = src.shape[0], src.shape[2]
+            dst = staged[4:P:8, first_col[name] : first_col[name] + z * c].bitcast(I32)
+            queue = nc.sync if n < 2 else nc.scalar
+            queue.dma_start(
+                out=dst.rearrange("q (z c) -> q z c", z=z),
+                in_=src.bitcast(I32).rearrange("z q c -> q z c"),
+            )
 
         wc = keep.tile([P, N], U32, align_bytes=64)
         cx = keep.tile([P, 2 * T], U8, align_bytes=64)
         wa = keep.tile([P, 2, 2 * N], U8, align_bytes=64)
         xa = keep.tile([P, 2, S], U32, align_bytes=64)
         wb = keep.tile([P, 2, 2 * N], U8, align_bytes=64)
-        xb_rows = xb.rearrange("(z p j) u -> z p j u", z=2, j=PACK)
-        raw0 = keep.tile([P, PACK, U], F32)
-        raw1a = keep.tile([P, PACK, HALF], F32)
-        raw1b = keep.tile([P, PACK, HALF], F32)
         nc.sync.dma_start(out=wc[:].bitcast(I32), in_=wc_words[0].rearrange("p c r -> p (c r)").bitcast(I32))
         nc.sync.dma_start(out=cx[:].bitcast(I32), in_=cx_words[0].bitcast(I32))
+        xb_rows = xb.rearrange("(z p j) u -> z p j u", z=2, j=PACK)
+        raw0 = keep.tile([P, PACK, U], F32)
+        nc.scalar.dma_start(out=raw0[:], in_=xb_rows[0])
+        for r in range(4):
+            nc.sync.dma_start(
+                out=planes[r:P:32, :].bitcast(I32),
+                in_=staged[4 + 8 * r : P : 32, :].bitcast(I32),
+            )
+        nc.sync.dma_start(out=wa[:].bitcast(I32), in_=wa_words.bitcast(I32).rearrange("z p c -> p z c"))
         nc.sync.dma_start(
             out=xa[:].bitcast(I32),
             in_=xa_words.rearrange("z p c r -> z p (c r)").bitcast(I32).rearrange("z p c -> p z c"),
         )
-        spread(0)
-        nc.sync.dma_start(out=wa[:].bitcast(I32), in_=wa_words.bitcast(I32).rearrange("z p c -> p z c"))
-        nc.sync.dma_start(out=raw0[:], in_=xb_rows[0])
-        spread(1)
+        raw = {}
+        for h in range(2):
+            raw[0, h] = raw0[:, :, HALF * h : HALF * (h + 1)]
+            raw1 = keep.tile([P, PACK, HALF], F32, name="raw1%d" % h)
+            nc.sync.dma_start(out=raw1[:], in_=xb_rows[1][:, :, HALF * h : HALF * (h + 1)])
+            raw[1, h] = raw1[:]
         nc.sync.dma_start(out=wb[:].bitcast(I32), in_=wb_words.bitcast(I32).rearrange("z p c -> p z c"))
-        nc.sync.dma_start(out=raw1a[:], in_=xb_rows[1][:, :, 0:HALF])
-        nc.sync.dma_start(out=raw1b[:], in_=xb_rows[1][:, :, HALF:U])
 
-        xq0 = keep.tile([P, U], U32, align_bytes=64)
-        xs0 = keep.tile([P, U], U8, align_bytes=64)
-        xq1 = keep.tile([P, U], U32, align_bytes=64)
-        xs1 = keep.tile([P, U], U8, align_bytes=64)
+        xq = [keep.tile([P, U], U32, align_bytes=64, name="xq%d" % z) for z in range(2)]
+        xs = [keep.tile([P, U], U8, align_bytes=64, name="xs%d" % z) for z in range(2)]
+        grouped = {}
+        for z in range(2):
+            for h in range(2):
+                grouped[z, h] = keep.tile([P, HALF, PACK], BF16, align_bytes=64, name="grouped%d%d" % (z, h))
 
-        def interleave(raw, cols, name):
-            grouped = keep.tile([P, cols, PACK], BF16, align_bytes=64, name=name)
-            nc.vector.tensor_copy(
-                out=grouped[:].rearrange("p (c i) t -> p c t i", i=4),
-                in_=raw[:].rearrange("p t (c i) -> p c t i", i=4),
+        def interleave(copy, z, h, c0, c1):
+            copy(
+                out=grouped[z, h][:, c0:c1, :].rearrange("p (c i) t -> p c t i", i=4),
+                in_=raw[z, h][:, :, c0:c1].rearrange("p t (c i) -> p c t i", i=4),
             )
-            return grouped
 
-        def quantize(grouped, codes, scales):
-            nc.vector.quantize_mx(out=codes.bitcast(FP8X4), scales=scales, in_=grouped[:].rearrange("p c t -> p (c t)"))
-
-        g0 = interleave(raw0, U, "g0")
-        quantize(g0, xq0[:], xs0[:])
-        g1a = interleave(raw1a, HALF, "g1a")
-        quantize(g1a, xq1[:, 0:HALF], xs1[:, 0:HALF])
-        g1b = interleave(raw1b, HALF, "g1b")
-        quantize(g1b, xq1[:, HALF:U], xs1[:, HALF:U])
+        def quantize(z, h):
+            cols = slice(HALF * h, HALF * (h + 1))
+            nc.vector.quantize_mx(
+                out=xq[z][:, cols].bitcast(FP8X4),
+                scales=xs[z][:, cols],
+                in_=grouped[z, h][:].rearrange("p c t -> p (c t)"),
+            )
 
         def plane(name, first, cols):
-            g, c0 = place[name]
-            return planes[g][:, c0 + first : c0 + first + cols]
+            c0 = first_col[name] + first
+            return planes[:, c0 : c0 + cols]
 
         def context_pass(acc, i, t0):
             nc.tensor.matmul_mx(
@@ -138,6 +133,10 @@ def tile_mix_two_batches_one_context_kernel(
 
         acc_a = [psum.tile([P, S], F32, name="acc_a%d" % i) for i in range(N_TILES)]
         acc_b = [psum.tile([P, U], F32, name="acc_b%d" % i) for i in range(N_TILES)]
+        for z in range(2):
+            for h in range(2):
+                interleave(nc.vector.tensor_copy, z, h, 0, HALF)
+                quantize(z, h)
         for i in range(N_TILES):
             context_pass(acc_a[i], i, 0)
         for i in range(N_TILES):
@@ -147,7 +146,6 @@ def tile_mix_two_batches_one_context_kernel(
                 batch_pass(acc_a[i], wa, "wa", i, z, xa[:, z, :], plane("xa", S * z, S))
             finish(acc_a[i], i, 0)
         for i in range(N_TILES):
-            batch_pass(acc_b[i], wb, "wb", i, 0, xq0[:], xs0[:])
-        for i in range(N_TILES):
-            batch_pass(acc_b[i], wb, "wb", i, 1, xq1[:], xs1[:])
+            for z in range(2):
+                batch_pass(acc_b[i], wb, "wb", i, z, xq[z][:], xs[z][:])
             finish(acc_b[i], i, S)

@@ -33,16 +33,18 @@ def tile_mix_two_batches_one_context_kernel(
         psum = ctx.enter_context(tc.psum_pool(name="psum", bufs=1))
         ctx.enter_context(tc.manual_schedule())
 
-        sources = [("wc", wc_scales), ("cx", cx_scales), ("wa", wa_scales), ("xa", xa_scales), ("wb", wb_scales)]
+        early = [("wc", wc_scales), ("cx", cx_scales), ("wa", wa_scales), ("xa", xa_scales)]
         first_col = {}
         width = 0
-        for name, src in sources:
+        for name, src in early:
             first_col[name] = width
             width = width + src.shape[0] * src.shape[2]
         staged = keep.tile([P, width], U8, align_bytes=64)
         planes = keep.tile([P, width], U8, align_bytes=64)
+        wb_planes = keep.tile([P, 2, N], U8, align_bytes=64)
         nc.vector.memset(planes[:].bitcast(I32), 0)
-        for n, (name, src) in enumerate(sources):
+        nc.vector.memset(wb_planes[:].bitcast(I32), 0)
+        for n, (name, src) in enumerate(early):
             z, c = src.shape[0], src.shape[2]
             dst = staged[4:P:8, first_col[name] : first_col[name] + z * c].bitcast(I32)
             queue = nc.sync if n < 2 else nc.scalar
@@ -56,27 +58,36 @@ def tile_mix_two_batches_one_context_kernel(
         wa = keep.tile([P, 2, 2 * N], U8, align_bytes=64)
         xa = keep.tile([P, 2, S], U32, align_bytes=64)
         wb = keep.tile([P, 2, 2 * N], U8, align_bytes=64)
+        xb_rows = xb.rearrange("(z p j) u -> z p j u", z=2, j=PACK)
+        raw = {}
+        for z in range(2):
+            for h in range(2):
+                raw[z, h] = keep.tile([P, PACK, HALF], F32, name="raw%d%d" % (z, h))
+
+        def load_xb(queue, z, h):
+            queue.dma_start(out=raw[z, h][:], in_=xb_rows[z][:, :, HALF * h : HALF * (h + 1)])
+
         nc.sync.dma_start(out=wc[:].bitcast(I32), in_=wc_words[0].rearrange("p c r -> p (c r)").bitcast(I32))
         nc.sync.dma_start(out=cx[:].bitcast(I32), in_=cx_words[0].bitcast(I32))
-        xb_rows = xb.rearrange("(z p j) u -> z p j u", z=2, j=PACK)
-        raw0 = keep.tile([P, PACK, U], F32)
-        nc.scalar.dma_start(out=raw0[:], in_=xb_rows[0])
+        nc.scalar.dma_start(out=wa[:].bitcast(I32), in_=wa_words.bitcast(I32).rearrange("z p c -> p z c"))
+        load_xb(nc.scalar, 0, 0)
         for r in range(4):
             nc.sync.dma_start(
                 out=planes[r:P:32, :].bitcast(I32),
                 in_=staged[4 + 8 * r : P : 32, :].bitcast(I32),
             )
-        nc.sync.dma_start(out=wa[:].bitcast(I32), in_=wa_words.bitcast(I32).rearrange("z p c -> p z c"))
         nc.sync.dma_start(
             out=xa[:].bitcast(I32),
             in_=xa_words.rearrange("z p c r -> z p (c r)").bitcast(I32).rearrange("z p c -> p z c"),
         )
-        raw = {}
-        for h in range(2):
-            raw[0, h] = raw0[:, :, HALF * h : HALF * (h + 1)]
-            raw1 = keep.tile([P, PACK, HALF], F32, name="raw1%d" % h)
-            nc.sync.dma_start(out=raw1[:], in_=xb_rows[1][:, :, HALF * h : HALF * (h + 1)])
-            raw[1, h] = raw1[:]
+        load_xb(nc.sync, 0, 1)
+        load_xb(nc.sync, 1, 0)
+        for r in range(4):
+            nc.sync.dma_start(
+                out=wb_planes[r:P:32].bitcast(I32),
+                in_=wb_scales.bitcast(I32)[:, r:16:4, :].rearrange("z q c -> q z c"),
+            )
+        load_xb(nc.sync, 1, 1)
         nc.sync.dma_start(out=wb[:].bitcast(I32), in_=wb_words.bitcast(I32).rearrange("z p c -> p z c"))
 
         xq = [keep.tile([P, U], U32, align_bytes=64, name="xq%d" % z) for z in range(2)]
@@ -88,8 +99,8 @@ def tile_mix_two_batches_one_context_kernel(
 
         def interleave(copy, z, h, c0, c1):
             copy(
-                out=grouped[z, h][:, c0:c1, :].rearrange("p (c i) t -> p c t i", i=4),
-                in_=raw[z, h][:, :, c0:c1].rearrange("p t (c i) -> p c t i", i=4),
+                out=grouped[z, h][:, c0:c1, :].rearrange("p (c i) t -> p c t i", i=2),
+                in_=raw[z, h][:, :, c0:c1].rearrange("p t (c i) -> p c t i", i=2),
             )
 
         def quantize(z, h):
@@ -101,6 +112,8 @@ def tile_mix_two_batches_one_context_kernel(
             )
 
         def plane(name, first, cols):
+            if name == "wb":
+                return wb_planes[:, first // N, first % N : first % N + cols]
             c0 = first_col[name] + first
             return planes[:, c0 : c0 + cols]
 
@@ -126,10 +139,12 @@ def tile_mix_two_batches_one_context_kernel(
                 stop=(z == 1),
             )
 
-        def finish(acc, i, t0):
-            y = keep.tile([P, S], F32, name="y_%d_%d" % (t0, i))
-            nc.scalar.activation(out=y[:], in_=acc[:], func=SILU)
-            nc.sync.dma_start(out=out[M_TILE * i : M_TILE * (i + 1), t0 : t0 + S], in_=y[:])
+        def finish(acc, i, t0, parts=1):
+            cols = S // parts
+            for c0 in range(0, S, cols):
+                y = keep.tile([P, cols], F32, name="y_%d_%d" % (t0 + c0, i))
+                nc.scalar.activation(out=y[:], in_=acc[:, c0 : c0 + cols], func=SILU)
+                nc.sync.dma_start(out=out[M_TILE * i : M_TILE * (i + 1), t0 + c0 : t0 + c0 + cols], in_=y[:])
 
         acc_a = [psum.tile([P, S], F32, name="acc_a%d" % i) for i in range(N_TILES)]
         acc_b = [psum.tile([P, U], F32, name="acc_b%d" % i) for i in range(N_TILES)]
@@ -140,12 +155,14 @@ def tile_mix_two_batches_one_context_kernel(
         for i in range(N_TILES):
             context_pass(acc_a[i], i, 0)
         for i in range(N_TILES):
-            context_pass(acc_b[i], i, S)
-        for i in range(N_TILES):
             for z in range(2):
                 batch_pass(acc_a[i], wa, "wa", i, z, xa[:, z, :], plane("xa", S * z, S))
             finish(acc_a[i], i, 0)
+        for i in range(N_TILES - 1):
+            context_pass(acc_b[i], i, S)
         for i in range(N_TILES):
+            if i == N_TILES - 1:
+                context_pass(acc_b[i], i, S)
             for z in range(2):
                 batch_pass(acc_b[i], wb, "wb", i, z, xq[z][:], xs[z][:])
-            finish(acc_b[i], i, S)
+            finish(acc_b[i], i, S, parts=2 if i == N_TILES - 1 else 1)

@@ -20,7 +20,7 @@ K_PASS = P * PACK
 M_TILE = 128
 N_TILES = N // M_TILE
 HALF = U // 2
-SPLIT = 160
+SPLIT = 176
 
 
 def tile_mix_two_batches_one_context_kernel(
@@ -148,21 +148,28 @@ def tile_mix_two_batches_one_context_kernel(
 
         acc_a = [psum.tile([P, S], F32, name="acc_a%d" % i) for i in range(N_TILES)]
         acc_b = [psum.tile([P, U], F32, name="acc_b%d" % i) for i in range(N_TILES)]
-        for z in range(2):
-            for h in range(2):
-                interleave(nc.vector.tensor_copy, z, h, 0, HALF)
-                quantize(z, h)
+        for z, h in ((0, 0), (0, 1), (1, 0)):
+            interleave(nc.vector.tensor_copy, z, h, 0, HALF)
+            quantize(z, h)
         for i in range(N_TILES):
             context_pass(acc_a[i], i, 0)
         for i in range(N_TILES):
             for z in range(2):
                 batch_pass(acc_a[i], wa, "wa", i, z, xa[:, z, :], plane("xa", S * z, S))
+            if i == N_TILES - 1:
+                interleave(nc.vector.tensor_copy, 1, 1, 0, SPLIT)
+                interleave(nc.scalar.copy, 1, 1, SPLIT, HALF)
+                quantize(1, 1)
             finish(acc_a[i], i, 0)
         for i in range(N_TILES - 1):
             context_pass(acc_b[i], i, S)
-        for i in range(N_TILES):
-            if i == N_TILES - 1:
-                context_pass(acc_b[i], i, S)
+        for z in range(2):
+            for i in range(2):
+                batch_pass(acc_b[i], wb, "wb", i, z, xq[z][:], xs[z][:])
+        for i in range(2):
+            finish(acc_b[i], i, S)
+        context_pass(acc_b[N_TILES - 1], N_TILES - 1, S)
+        for i in range(2, N_TILES):
             for z in range(2):
                 batch_pass(acc_b[i], wb, "wb", i, z, xq[z][:], xs[z][:])
             finish(acc_b[i], i, S, parts=2 if i == N_TILES - 1 else 1)

@@ -44,11 +44,10 @@ def tile_mix_two_batches_one_context_kernel(
         wb_planes = keep.tile([P, 2, N], U8, align_bytes=64)
         nc.vector.memset(planes[:].bitcast(I32), 0)
         nc.vector.memset(wb_planes[:].bitcast(I32), 0)
-        for n, (name, src) in enumerate(early):
+        for name, src in early:
             z, c = src.shape[0], src.shape[2]
             dst = staged[4:P:8, first_col[name] : first_col[name] + z * c].bitcast(I32)
-            queue = nc.sync if n < 2 else nc.scalar
-            queue.dma_start(
+            nc.scalar.dma_start(
                 out=dst.rearrange("q (z c) -> q z c", z=z),
                 in_=src.bitcast(I32).rearrange("z q c -> q z c"),
             )

from contextlib import ExitStack

import concourse.mybir as mybir

K, L, S, U, T, N = 1024, 512, 512, 512, 1024, 512
FLOPS = 2 * N * (K * S + K * U + L * T)

F32 = mybir.dt.float32
BF16 = mybir.dt.bfloat16
I32 = mybir.dt.int32
U32 = mybir.dt.uint32
U8 = mybir.dt.uint8
FP8X4 = mybir.dt.float8_e4m3fn_x4
FP4X4 = mybir.dt.float4_e2m1fn_x4
SILU = mybir.ActivationFunctionType.Silu

P = 128
PACK = 4
K_PASS = P * PACK
M_TILE = 128
N_TILES = N // M_TILE
HALF = U // 2
SPLIT = 176


def tile_mix_two_batches_one_context_kernel(
    tc, xa_words, xa_scales, wa_words, wa_scales, xb, wb_words, wb_scales,
    cx_words, cx_scales, wc_words, wc_scales, out
):
    nc = tc.nc
    with ExitStack() as ctx:
        keep = ctx.enter_context(tc.tile_pool(name="keep", bufs=1))
        psum = ctx.enter_context(tc.psum_pool(name="psum", bufs=1))
        ctx.enter_context(tc.manual_schedule())

        early = [("wc", wc_scales), ("cx", cx_scales), ("wa", wa_scales), ("xa", xa_scales)]
        first_col = {}
        width = 0
        for name, src in early:
            first_col[name] = width
            width = width + src.shape[0] * src.shape[2]
        staged = keep.tile([P, width], U8, align_bytes=64)
        planes = keep.tile([P, width], U8, align_bytes=64)
        wb_planes = keep.tile([P, 2, N], U8, align_bytes=64)
        nc.vector.memset(planes[:].bitcast(I32), 0)
        nc.vector.memset(wb_planes[:].bitcast(I32), 0)
        for name, src in early:
            z, c = src.shape[0], src.shape[2]
            dst = staged[4:P:8, first_col[name] : first_col[name] + z * c].bitcast(I32)
            nc.scalar.dma_start(
                out=dst.rearrange("q (z c) -> q z c", z=z),
                in_=src.bitcast(I32).rearrange("z q c -> q z c"),
            )

        wc = keep.tile([P, N], U32, align_bytes=64)
        cx = keep.tile([P, 2 * T], U8, align_bytes=64)
        wa = keep.tile([P, 2, 2 * N], U8, align_bytes=64)
        xa = keep.tile([P, 2, S], U32, align_bytes=64)
        wb = keep.tile([P, 2, 2 * N], U8, align_bytes=64)
        xb_rows = xb.rearrange("(z p j) u -> z p j u", z=2, j=PACK)
        raw = {}
        for z in range(2):
            for h in range(2):
                raw[z, h] = keep.tile([P, PACK, HALF], F32, name="raw%d%d" % (z, h))

        def load_xb(queue, z, h):
            queue.dma_start(out=raw[z, h][:], in_=xb_rows[z][:, :, HALF * h : HALF * (h + 1)])

        nc.sync.dma_start(out=wc[:].bitcast(I32), in_=wc_words[0].rearrange("p c r -> p (c r)").bitcast(I32))
        nc.sync.dma_start(out=cx[:].bitcast(I32), in_=cx_words[0].bitcast(I32))
        nc.scalar.dma_start(out=wa[:].bitcast(I32), in_=wa_words.bitcast(I32).rearrange("z p c -> p z c"))
        load_xb(nc.scalar, 0, 0)
        for r in range(4):
            nc.sync.dma_start(
                out=planes[r:P:32, :].bitcast(I32),
                in_=staged[4 + 8 * r : P : 32, :].bitcast(I32),
            )
        nc.sync.dma_start(
            out=xa[:].bitcast(I32),
            in_=xa_words.rearrange("z p c r -> z p (c r)").bitcast(I32).rearrange("z p c -> p z c"),
        )
        load_xb(nc.sync, 0, 1)
        load_xb(nc.sync, 1, 0)
        for r in range(4):
            nc.sync.dma_start(
                out=wb_planes[r:P:32].bitcast(I32),
                in_=wb_scales.bitcast(I32)[:, r:16:4, :].rearrange("z q c -> q z c"),
            )
        load_xb(nc.sync, 1, 1)
        nc.sync.dma_start(out=wb[:].bitcast(I32), in_=wb_words.bitcast(I32).rearrange("z p c -> p z c"))

        xq = [keep.tile([P, U], U32, align_bytes=64, name="xq%d" % z) for z in range(2)]
        xs = [keep.tile([P, U], U8, align_bytes=64, name="xs%d" % z) for z in range(2)]
        grouped = {}
        for z in range(2):
            for h in range(2):
                grouped[z, h] = keep.tile([P, HALF, PACK], BF16, align_bytes=64, name="grouped%d%d" % (z, h))

        def interleave(copy, z, h, c0, c1):
            copy(
                out=grouped[z, h][:, c0:c1, :].rearrange("p (c i) t -> p c t i", i=2),
                in_=raw[z, h][:, :, c0:c1].rearrange("p t (c i) -> p c t i", i=2),
            )

        def quantize(z, h):
            cols = slice(HALF * h, HALF * (h + 1))
            nc.vector.quantize_mx(
                out=xq[z][:, cols].bitcast(FP8X4),
                scales=xs[z][:, cols],
                in_=grouped[z, h][:].rearrange("p c t -> p (c t)"),
            )

        def plane(name, first, cols):
            if name == "wb":
                return wb_planes[:, first // N, first % N : first % N + cols]
            c0 = first_col[name] + first
            return planes[:, c0 : c0 + cols]

        def context_pass(acc, i, t0):
            nc.tensor.matmul_mx(
                out=acc[:],
                lhsT=wc[:, M_TILE * i : M_TILE * (i + 1)].bitcast(FP8X4),
                lhsT_scale=plane("wc", M_TILE * i, M_TILE),
                rhs=cx[:, 2 * t0 : 2 * (t0 + S)].bitcast(FP4X4),
                rhs_scale=plane("cx", t0, S),
                start=True,
                stop=False,
            )

        def batch_pass(acc, w, w_name, i, z, codes, scales):
            nc.tensor.matmul_mx(
                out=acc[:],
                lhsT=w[:, z, 2 * M_TILE * i : 2 * M_TILE * (i + 1)].bitcast(FP4X4),
                lhsT_scale=plane(w_name, N * z + M_TILE * i, M_TILE),
                rhs=codes.bitcast(FP8X4),
                rhs_scale=scales,
                start=False,
                stop=(z == 1),
            )

        def finish(acc, i, t0, parts=1):
            cols = S // parts
            for c0 in range(0, S, cols):
                y = keep.tile([P, cols], F32, name="y_%d_%d" % (t0 + c0, i))
                nc.scalar.activation(out=y[:], in_=acc[:, c0 : c0 + cols], func=SILU)
                nc.sync.dma_start(out=out[M_TILE * i : M_TILE * (i + 1), t0 + c0 : t0 + c0 + cols], in_=y[:])

        acc_a = [psum.tile([P, S], F32, name="acc_a%d" % i) for i in range(N_TILES)]
        acc_b = [psum.tile([P, U], F32, name="acc_b%d" % i) for i in range(N_TILES)]
        for z, h in ((0, 0), (0, 1), (1, 0)):
            interleave(nc.vector.tensor_copy, z, h, 0, HALF)
            quantize(z, h)
        for i in range(N_TILES):
            context_pass(acc_a[i], i, 0)
        for i in range(N_TILES):
            for z in range(2):
                batch_pass(acc_a[i], wa, "wa", i, z, xa[:, z, :], plane("xa", S * z, S))
            if i == N_TILES - 1:
                interleave(nc.vector.tensor_copy, 1, 1, 0, SPLIT)
                interleave(nc.scalar.copy, 1, 1, SPLIT, HALF)
                quantize(1, 1)
            finish(acc_a[i], i, 0)
        for i in range(N_TILES - 1):
            context_pass(acc_b[i], i, S)
        for z in range(2):
            for i in range(2):
                batch_pass(acc_b[i], wb, "wb", i, z, xq[z][:], xs[z][:])
        for i in range(2):
            finish(acc_b[i], i, S)
        context_pass(acc_b[N_TILES - 1], N_TILES - 1, S)
        for i in range(2, N_TILES):
            for z in range(2):
                batch_pass(acc_b[i], wb, "wb", i, z, xq[z][:], xs[z][:])
            finish(acc_b[i], i, S, parts=2 if i == N_TILES - 1 else 1)
